import numpy as np
import ml_dtypes


def mxq(x, axis, fmt="e4m3"):
    dtype, down = {"e4m3": (ml_dtypes.float8_e4m3fn, 7), "e5m2": (ml_dtypes.float8_e5m2, 14)}[fmt]
    v = np.moveaxis(np.asarray(x, np.float32).astype(ml_dtypes.bfloat16).astype(np.float64), axis, -1)
    blocks = v.reshape(v.shape[:-1] + (-1, 32))
    amax = np.abs(blocks).max(-1, keepdims=True)
    byte = np.maximum(np.where(amax > 0, np.frexp(amax)[1] - 1 + 127, 0) - down, 1)
    scale = np.exp2(byte - 127.0)
    codes = (blocks / scale).astype(np.float32).astype(dtype).astype(np.float64)
    return np.moveaxis((codes * scale).reshape(v.shape), -1, axis)


WIDE = False


def mx_kscale(k):
    if not WIDE:
        return np.ones(k)
    levels = np.array([10, -10, 5, -5, 0])
    if k % 512:
        return np.exp2(np.random.permutation(np.resize(levels, k // 32))).repeat(32)
    a = np.empty((k // 512, 16))
    for p in range(k // 512):
        a[p, :8] = np.random.permutation(np.resize(levels, 8))
        for g in range(8):
            far = levels[np.abs(levels - a[p, g]) >= 10]
            a[p, g + 8] = far[np.random.randint(len(far))]
    return np.exp2(a.ravel()).repeat(32)


def f64(x):
    return np.asarray(x).astype(np.float64)


def striped(idx):
    return np.tile(idx.reshape(-1, 16).T, (8, 1)).astype(np.uint16)


def unstriped(offs):
    return offs[:16].T.reshape(-1).astype(np.int64)


def pack_weight(w):
    k, n = w.shape
    w = f64(np.asarray(w, np.float32).astype(ml_dtypes.bfloat16)).reshape(k // 32, 32, n)
    amax = np.abs(w).max(1)
    byte = np.clip(np.where(amax > 0, np.frexp(amax)[1] - 1 + 127 - 7, 1), 1, 254)
    scaled = (w * np.exp2(127.0 - byte)[:, None, :]).reshape(k, n).astype(np.float32)
    words = np.ascontiguousarray(scaled.reshape(k // 512, 128, 4, n).transpose(0, 1, 3, 2)).astype(ml_dtypes.float8_e4m3fn).view(np.uint8)
    return words, np.ascontiguousarray(byte.astype(np.uint8).reshape(k // 512, 16, n))


def unpack_weight(words, scales):
    g, p, n, _ = words.shape
    vals = np.ascontiguousarray(words).view(ml_dtypes.float8_e4m3fn).astype(np.float64) * np.repeat(np.exp2(scales.astype(np.float64) - 127.0), 8, axis=1)[..., None]
    return vals.transpose(0, 1, 3, 2).reshape(g * 512, n)


K, T, S, V = 1024, 2048, 512, 512
P = 2 ** 7


def setup_inputs():
    n = np.random.standard_normal
    s = mx_kscale(K)[:, None]
    packed_xT = pack_weight(n((K, T)) * s)
    return {
        "x_words": packed_xT[0],
        "x_scales": packed_xT[1],
        "hT": (n((K, V)) / np.sqrt(K) / s).astype(np.float32),
        "ratio": (np.random.uniform(0.0, 2.0, (V, S)) ** 2).astype(np.float32),
        "rate": (np.tile(np.random.uniform(0.3, 1.5, S), (P, 1))).astype(np.float32),
        "offs": striped(np.random.permutation(T)[:S]),
    }


def reference(x_words, x_scales, hT, ratio, rate, offs):
    hTq = mxq(f64(hT), 0, "e4m3")
    xq = unpack_weight(x_words, x_scales)[:, unstriped(offs)]
    y = 0.7 * (hTq.T @ xq)
    sc = np.exp(y)
    return f64(rate)[:1] * (sc - (f64(ratio) * y) + f64(ratio) * (np.log(f64(ratio) + 0.05) - 1.0))

@@ -1,0 +1,151 @@
+from contextlib import ExitStack
+
+import concourse.mybir as mybir
+from concourse.masks import make_identity
+
+K, T, S, V = 1024, 2048, 512, 512
+FLOPS = 2 * K * V * S
+
+F32 = mybir.dt.float32
+BF16 = mybir.dt.bfloat16
+I32 = mybir.dt.int32
+U32 = mybir.dt.uint32
+U16 = mybir.dt.uint16
+U8 = mybir.dt.uint8
+FP8X4 = mybir.dt.float8_e4m3fn_x4
+ACT = mybir.ActivationFunctionType
+ALU = mybir.AluOpType
+
+P = 128
+PACK = 4
+PASSES = K // (P * PACK)
+TILES = V // P
+HALF = V // 2
+
+
+def tile_picked_ysedd_loss_p_kernel(
+    tc, x_words, x_scales, hT, ratio, rate, offs, out
+):
+    nc = tc.nc
+    with ExitStack() as ctx:
+        keep = ctx.enter_context(tc.tile_pool(name="keep", bufs=1))
+        psum = ctx.enter_context(tc.psum_pool(name="psum", bufs=1))
+
+        def load_ratio(h):
+            tile = keep.tile([P, 2, S], F32, name=f"ratio{h}")
+            nc.sync.dma_start(tile[:], ratio[h * HALF : (h + 1) * HALF, :].rearrange("(m p) j -> p m j", p=P))
+            return tile
+
+        def load_scale_rows():
+            for q in range(4):
+                nc.sync.dma_start(scale_rows[32 * q : 32 * q + 8, :], x_scales.bitcast(I32)[:, 4 * q : 4 * q + 4, :])
+
+        def load_words(g):
+            tile = keep.tile([P, T], U32, name=f"word_table{g}", align_bytes=64)
+            nc.sync.dma_start(tile[:].bitcast(I32), x_words[g].rearrange("p n t -> p (n t)").bitcast(I32))
+            return tile
+
+        def load_hidden(first, count):
+            for g in range(PASSES):
+                raw = keep.tile([P, PACK, count * P], F32, name=f"h_raw{first}{g}")
+                rows = hT[g * 512 : (g + 1) * 512, first * P : (first + count) * P]
+                nc.sync.dma_start(raw[:], rows.rearrange("(p j) c -> p j c", j=PACK))
+                for i in range(count):
+                    h_raw[first + i, g] = raw[:, :, i * P : (i + 1) * P]
+
+        offsets = keep.tile([P, S // 16], U16, name="offsets")
+        scale_rows = keep.tile([P, T // 4], I32, name="scale_rows")
+        rate_col = keep.tile([P, 4], F32, name="rate_col")
+        h_raw = {}
+        nc.sync.dma_start(offsets[:], offs)
+        ratio_sb = [load_ratio(0), load_ratio(1)]
+        word_table = [load_words(0)]
+        load_scale_rows()
+        load_hidden(0, 1)
+        word_table.append(load_words(1))
+        nc.sync.dma_start(rate_col[:], rate[0:1, :].rearrange("o (p b) -> (o p) b", b=4))
+        load_hidden(1, 1)
+        load_hidden(2, 2)
+
+        scale_table = keep.tile([P, T], U8, name="scale_table", align_bytes=64)
+        nc.vector.memset(scale_table[:].bitcast(I32), 0)
+        identity = keep.tile([P, P], F32, name="identity")
+        make_identity(nc, identity[:])
+        for q in range(4):
+            rows = slice(32 * q, 32 * q + 8)
+            nc.vector.tensor_copy(scale_table[:].bitcast(I32)[rows, :], scale_rows[rows, :])
+
+        rate_bank = psum.tile([P, 4, P], F32, name="rate_bank")
+        for b in range(4):
+            nc.tensor.transpose(rate_bank[:, b, :], rate_col[:, b : b + 1].to_broadcast([P, P]), identity[:])
+
+        log_sb = []
+        for h in range(2):
+            lg = keep.tile([P, 2, S], F32, name=f"log{h}")
+            nc.scalar.activation(lg[:], ratio_sb[h][:], ACT.Ln, bias=0.05)
+            log_sb.append(lg)
+        warm = keep.tile([P, 1], F32, name="warm")
+        nc.scalar.activation(warm[:], log_sb[1][:, 1, S - 1 : S], ACT.Exp)
+
+        x_scale = keep.tile([P, S], U8, name="x_scale", align_bytes=64)
+        x_code = []
+        for g in range(PASSES):
+            c = keep.tile([P, S], U32, name=f"x_code{g}", align_bytes=64)
+            nc.vector.tensor_copy(c[:], word_table[g][:].indirect(offsets[:]))
+            x_code.append(c)
+            if g == 0:
+                nc.vector.tensor_copy(x_scale[:], scale_table[:].indirect(offsets[:]))
+
+        def product(m):
+            acc = psum.tile([P, S], F32, name=f"acc{m}")
+            for g in range(PASSES):
+                grouped = keep.tile([P, P, PACK], BF16, name=f"grouped{m}{g}", align_bytes=64)
+                src = h_raw[m, g].rearrange("p t (c i) -> p c t i", i=4)
+                dst = grouped[:].rearrange("p (c i) t -> p c t i", i=4)
+                if m == 0:
+                    nc.vector.tensor_copy(dst, src)
+                else:
+                    nc.scalar.copy(dst, src)
+                h_code = keep.tile([P, P], U32, name=f"h_code{m}{g}", align_bytes=64)
+                h_scale = keep.tile([P, P], U8, name=f"h_scale{m}{g}", align_bytes=64)
+                nc.vector.quantize_mx(
+                    out=h_code[:].bitcast(FP8X4), scales=h_scale[:], in_=grouped[:].rearrange("p c t -> p (c t)")
+                )
+                nc.tensor.matmul_mx(
+                    out=acc[:],
+                    lhsT=h_code[:].bitcast(FP8X4),
+                    lhsT_scale=h_scale[:],
+                    rhs=x_code[g][:].bitcast(FP8X4),
+                    rhs_scale=x_scale[4 * g : P, :],
+                    start=(g == 0),
+                    stop=(g == PASSES - 1),
+                )
+            return acc
+
+        def finish(m, acc, lo, hi, adder):
+            h, i = divmod(m, 2)
+            n = hi - lo
+            sc = keep.tile([P, n], F32, name=f"sc{m}_{lo}")
+            nc.scalar.activation(sc[:], acc[:, lo:hi], ACT.Exp, scale=0.7)
+            gap = keep.tile([P, n], F32, name=f"gap{m}_{lo}")
+            nc.vector.scalar_tensor_tensor(gap[:], acc[:, lo:hi], -0.7, log_sb[h][:, i, lo:hi], ALU.mult, ALU.add)
+            term = keep.tile([P, n], F32, name=f"term{m}_{lo}")
+            nc.vector.scalar_tensor_tensor(term[:], gap[:], -1.0, ratio_sb[h][:, i, lo:hi], ALU.add, ALU.mult)
+            total = keep.tile([P, n], F32, name=f"total{m}_{lo}")
+            adder.tensor_tensor(total[:], term[:], sc[:], ALU.add)
+            res = keep.tile([P, n], F32, name=f"res{m}_{lo}")
+            nc.vector.tensor_tensor(
+                res[:].rearrange("p (c b) -> p c b", b=4),
+                total[:].rearrange("p (c b) -> p c b", b=4),
+                rate_bank[:, :, lo // 4 : hi // 4].rearrange("p b c -> p c b"),
+                ALU.mult,
+            )
+            nc.sync.dma_start(out[m * P : (m + 1) * P, lo:hi], res[:])
+
+        for m in range(TILES):
+            acc = product(m)
+            if m < TILES - 1:
+                finish(m, acc, 0, S, nc.gpsimd)
+            else:
+                finish(m, acc, 0, S // 2, nc.vector)
+                finish(m, acc, S // 2, S, nc.vector)

@@ -45,27 +45,26 @@ def tile_picked_ysedd_loss_p_kernel(
             nc.sync.dma_start(tile[:].bitcast(I32), x_words[g].rearrange("p n t -> p (n t)").bitcast(I32))
             return tile
 
-        def load_hidden(first, count):
-            for g in range(PASSES):
-                raw = keep.tile([P, PACK, count * P], F32, name=f"h_raw{first}{g}")
-                rows = hT[g * 512 : (g + 1) * 512, first * P : (first + count) * P]
-                nc.sync.dma_start(raw[:], rows.rearrange("(p j) c -> p j c", j=PACK))
-                for i in range(count):
-                    h_raw[first + i, g] = raw[:, :, i * P : (i + 1) * P]
+        def load_hidden(g, first, count):
+            raw = keep.tile([P, PACK, count * P], F32, name=f"h_raw{first}{g}", tag=f"raw{first}{g}")
+            rows = hT[g * 512 : (g + 1) * 512, first * P : (first + count) * P]
+            nc.sync.dma_start(raw[:], rows.rearrange("(p j) c -> p j c", j=PACK))
+            for i in range(count):
+                h_raw[first + i, g] = raw[:, :, i * P : (i + 1) * P]
 
         offsets = keep.tile([P, S // 16], U16, name="offsets")
         scale_rows = keep.tile([P, T // 4], I32, name="scale_rows")
-        rate_col = keep.tile([P, 4], F32, name="rate_col")
+        rate_sb = keep.tile([P, S], F32, name="rate_sb")
         h_raw = {}
         nc.sync.dma_start(offsets[:], offs)
-        ratio_sb = [load_ratio(0), load_ratio(1)]
-        word_table = [load_words(0)]
         load_scale_rows()
-        load_hidden(0, 1)
+        ratio_sb = [load_ratio(0), load_ratio(1)]
+        load_hidden(0, 0, 4)
+        word_table = [load_words(0)]
         word_table.append(load_words(1))
-        nc.sync.dma_start(rate_col[:], rate[0:1, :].rearrange("o (p b) -> (o p) b", b=4))
-        load_hidden(1, 1)
-        load_hidden(2, 2)
+        load_hidden(1, 0, 2)
+        load_hidden(1, 2, 2)
+        nc.sync.dma_start(rate_sb[:], rate)
 
         scale_table = keep.tile([P, T], U8, name="scale_table", align_bytes=64)
         nc.vector.memset(scale_table[:].bitcast(I32), 0)
@@ -74,35 +73,49 @@ def tile_picked_ysedd_loss_p_kernel(
         for q in range(4):
             rows = slice(32 * q, 32 * q + 8)
             nc.vector.tensor_copy(scale_table[:].bitcast(I32)[rows, :], scale_rows[rows, :])
-
-        rate_bank = psum.tile([P, 4, P], F32, name="rate_bank")
-        for b in range(4):
-            nc.tensor.transpose(rate_bank[:, b, :], rate_col[:, b : b + 1].to_broadcast([P, P]), identity[:])
-
-        log_sb = []
-        for h in range(2):
-            lg = keep.tile([P, 2, S], F32, name=f"log{h}")
-            nc.scalar.activation(lg[:], ratio_sb[h][:], ACT.Ln, bias=0.05)
-            log_sb.append(lg)
-        warm = keep.tile([P, 1], F32, name="warm")
-        nc.scalar.activation(warm[:], log_sb[1][:, 1, S - 1 : S], ACT.Exp)
-
         x_scale = keep.tile([P, S], U8, name="x_scale", align_bytes=64)
+        nc.vector.tensor_copy(x_scale[:], scale_table[:].indirect(offsets[:]))
+
+        def turn_into(bank, source, start, stop):
+            for b in range(4):
+                nc.tensor.matmul(
+                    bank[:, b, :], source[:, b, :], identity[:], is_transpose=True,
+                    start=start and b == 0, stop=stop and b == 3,
+                )
+
+        stage = []
+        for m in range(TILES):
+            h, i = divmod(m, 2)
+            stage.append(psum.tile([P, 4, P], F32, name=f"stage{m}", tag="work", bufs=4))
+            turn_into(stage[m], ratio_sb[h][:, i, :].rearrange("p (b c) -> p b c", b=4), True, True)
+        ratio_t = []
+        sums = []
+        for m in range(TILES):
+            lg = keep.tile([P, 4, P], F32, name=f"log{m}")
+            nc.scalar.activation(lg[:], stage[m][:], ACT.Ln, bias=0.05)
+            rt = keep.tile([P, 4, P], F32, name=f"ratio_t{m}")
+            nc.scalar.copy(rt[:], stage[m][:])
+            fixed = keep.tile([P, 4, P], F32, name=f"fixed{m}")
+            nc.vector.scalar_tensor_tensor(fixed[:], lg[:], -1.0, rt[:], ALU.add, ALU.mult)
+            total = psum.tile([P, 4, P], F32, name=f"sum{m}")
+            turn_into(total, fixed, True, False)
+            ratio_t.append(rt)
+            sums.append(total)
+        warm = keep.tile([P, 1], F32, name="warm")
+        nc.scalar.activation(warm[:], lg[:, 3, P - 1 : P], ACT.Exp)
+
         x_code = []
         for g in range(PASSES):
             c = keep.tile([P, S], U32, name=f"x_code{g}", align_bytes=64)
             nc.vector.tensor_copy(c[:], word_table[g][:].indirect(offsets[:]))
             x_code.append(c)
-            if g == 0:
-                nc.vector.tensor_copy(x_scale[:], scale_table[:].indirect(offsets[:]))
 
-        def product(m):
-            acc = psum.tile([P, S], F32, name=f"acc{m}")
-            for g in range(PASSES):
-                grouped = keep.tile([P, P, PACK], BF16, name=f"grouped{m}{g}", align_bytes=64)
+        def product(m, g, acc):
+            if True:
+                grouped = keep.tile([P, P, PACK], BF16, name=f"grouped{m}{g}", tag=f"slot{m}{g}", align_bytes=64)
                 src = h_raw[m, g].rearrange("p t (c i) -> p c t i", i=4)
                 dst = grouped[:].rearrange("p (c i) t -> p c t i", i=4)
-                if m == 0:
+                if m + 2 * g < 2 or (m, g) == (0, 1):
                     nc.vector.tensor_copy(dst, src)
                 else:
                     nc.scalar.copy(dst, src)
@@ -111,41 +124,37 @@ def tile_picked_ysedd_loss_p_kernel(
                 nc.vector.quantize_mx(
                     out=h_code[:].bitcast(FP8X4), scales=h_scale[:], in_=grouped[:].rearrange("p c t -> p (c t)")
                 )
-                nc.tensor.matmul_mx(
-                    out=acc[:],
-                    lhsT=h_code[:].bitcast(FP8X4),
-                    lhsT_scale=h_scale[:],
-                    rhs=x_code[g][:].bitcast(FP8X4),
-                    rhs_scale=x_scale[4 * g : P, :],
-                    start=(g == 0),
-                    stop=(g == PASSES - 1),
-                )
-            return acc
+                for b in range(4):
+                    cols = slice(b * P, (b + 1) * P)
+                    nc.tensor.matmul_mx(
+                        out=acc[:, b, :],
+                        lhsT=x_code[g][:, cols].bitcast(FP8X4),
+                        lhsT_scale=x_scale[4 * g : P, cols],
+                        rhs=h_code[:].bitcast(FP8X4),
+                        rhs_scale=h_scale[:],
+                        start=(g == 0 and b == 0),
+                        stop=(g == PASSES - 1 and b == 3),
+                    )
 
-        def finish(m, acc, lo, hi, adder):
-            h, i = divmod(m, 2)
-            n = hi - lo
-            sc = keep.tile([P, n], F32, name=f"sc{m}_{lo}")
-            nc.scalar.activation(sc[:], acc[:, lo:hi], ACT.Exp, scale=0.7)
-            gap = keep.tile([P, n], F32, name=f"gap{m}_{lo}")
-            nc.vector.scalar_tensor_tensor(gap[:], acc[:, lo:hi], -0.7, log_sb[h][:, i, lo:hi], ALU.mult, ALU.add)
-            term = keep.tile([P, n], F32, name=f"term{m}_{lo}")
-            nc.vector.scalar_tensor_tensor(term[:], gap[:], -1.0, ratio_sb[h][:, i, lo:hi], ALU.add, ALU.mult)
-            total = keep.tile([P, n], F32, name=f"total{m}_{lo}")
-            adder.tensor_tensor(total[:], term[:], sc[:], ALU.add)
-            res = keep.tile([P, n], F32, name=f"res{m}_{lo}")
-            nc.vector.tensor_tensor(
-                res[:].rearrange("p (c b) -> p c b", b=4),
-                total[:].rearrange("p (c b) -> p c b", b=4),
-                rate_bank[:, :, lo // 4 : hi // 4].rearrange("p b c -> p c b"),
-                ALU.mult,
-            )
-            nc.sync.dma_start(out[m * P : (m + 1) * P, lo:hi], res[:])
+        def add_terms(m, acc):
+            cross = keep.tile([P, 4, P], F32, name=f"cross{m}")
+            nc.vector.scalar_tensor_tensor(cross[:], acc[:], -0.7, ratio_t[m][:], ALU.mult, ALU.mult)
+            sc = keep.tile([P, 4, P], F32, name=f"sc{m}", tag="raw21" if m == 0 else f"sc{m}")
+            nc.scalar.activation(sc[:], acc[:], ACT.Exp, scale=0.7)
+            turn_into(sums[m], cross, False, False)
+            turn_into(sums[m], sc, False, True)
 
+        def store(m):
+            res = keep.tile([P, S], F32, name=f"res{m}", tag="slot31" if m == 0 else f"res{m}", align_bytes=64)
+            nc.vector.tensor_tensor(res[:], sums[m][:].rearrange("p b c -> p (b c)"), rate_sb[:], ALU.mult)
+            nc.sync.dma_start(out[m * P : (m + 1) * P, :], res[:])
+
+        acc = [psum.tile([P, 4, P], F32, name=f"acc{m}", tag="work", bufs=4) for m in range(TILES)]
+        for g in range(PASSES):
+            for m in range(TILES):
+                product(m, g, acc[m])
         for m in range(TILES):
-            acc = product(m)
-            if m < TILES - 1:
-                finish(m, acc, 0, S, nc.gpsimd)
-            else:
-                finish(m, acc, 0, S // 2, nc.vector)
-                finish(m, acc, S // 2, S, nc.vector)
+            add_terms(m, acc[m])
+            if m > 0:
+                store(m - 1)
+        store(TILES - 1)

@@ -41,29 +41,25 @@ def tile_picked_ysedd_loss_p_kernel(
                 nc.sync.dma_start(scale_rows[32 * q : 32 * q + 8, :], x_scales.bitcast(I32)[:, 4 * q : 4 * q + 4, :])
 
         def load_words(g):
-            tile = keep.tile([P, T], U32, name=f"word_table{g}", align_bytes=64)
+            tile = keep.tile([P, T], U32, name=f"word_table{g}", tag=f"words{g}", align_bytes=64)
             nc.sync.dma_start(tile[:].bitcast(I32), x_words[g].rearrange("p n t -> p (n t)").bitcast(I32))
             return tile
 
         def load_hidden(g, first, count):
-            raw = keep.tile([P, PACK, count * P], F32, name=f"h_raw{first}{g}", tag=f"raw{first}{g}")
+            raw = keep.tile([P, PACK, count * P], F32, name=f"h_raw{first}{g}", tag=f"raw{first}{g}", align_bytes=64)
             rows = hT[g * 512 : (g + 1) * 512, first * P : (first + count) * P]
             nc.sync.dma_start(raw[:], rows.rearrange("(p j) c -> p j c", j=PACK))
-            for i in range(count):
-                h_raw[first + i, g] = raw[:, :, i * P : (i + 1) * P]
+            return raw[:]
 
         offsets = keep.tile([P, S // 16], U16, name="offsets")
         scale_rows = keep.tile([P, T // 4], I32, name="scale_rows")
         rate_sb = keep.tile([P, S], F32, name="rate_sb")
-        h_raw = {}
-        nc.sync.dma_start(offsets[:], offs)
         load_scale_rows()
+        nc.sync.dma_start(offsets[:], offs)
         ratio_sb = [load_ratio(0), load_ratio(1)]
-        load_hidden(0, 0, 4)
-        word_table = [load_words(0)]
-        word_table.append(load_words(1))
-        load_hidden(1, 0, 2)
-        load_hidden(1, 2, 2)
+        h_first = load_hidden(0, 0, 4)
+        word_table = [load_words(0), load_words(1)]
+        h_second = [load_hidden(1, 0, 2), load_hidden(1, 2, 2)]
         nc.sync.dma_start(rate_sb[:], rate)
 
         scale_table = keep.tile([P, T], U8, name="scale_table", align_bytes=64)
@@ -76,11 +72,40 @@ def tile_picked_ysedd_loss_p_kernel(
         x_scale = keep.tile([P, S], U8, name="x_scale", align_bytes=64)
         nc.vector.tensor_copy(x_scale[:], scale_table[:].indirect(offsets[:]))
 
+        def quantise(raw, copy, name, grouped_tag, code_tag):
+            width = raw.shape[2]
+            grouped = keep.tile([P, width, PACK], BF16, name=f"grouped_{name}", tag=grouped_tag, align_bytes=64)
+            copy(grouped[:].rearrange("p (c i) t -> p c t i", i=4), raw.rearrange("p t (c i) -> p c t i", i=4))
+            code = keep.tile([P, width], U32, name=f"h_code_{name}", tag=code_tag, align_bytes=64)
+            scale = keep.tile([P, width], U8, name=f"h_scale_{name}", align_bytes=64)
+            nc.vector.quantize_mx(
+                out=code[:].bitcast(FP8X4), scales=scale[:], in_=grouped[:].rearrange("p c t -> p (c t)")
+            )
+            return [(code[:, i : i + P], scale[:, i : i + P]) for i in range(0, width, P)]
+
+        def gather_words(g, tag):
+            code = keep.tile([P, S], U32, name=f"x_code{g}", tag=tag, align_bytes=64)
+            nc.vector.tensor_copy(code[:], word_table[g][:].indirect(offsets[:]))
+            return code
+
         def turn_into(bank, source, start, stop):
             for b in range(4):
                 nc.tensor.matmul(
                     bank[:, b, :], source[:, b, :], identity[:], is_transpose=True,
                     start=start and b == 0, stop=stop and b == 3,
+                )
+
+        def multiply(acc, g, x_code, h_code, h_scale):
+            for b in range(4):
+                cols = slice(b * P, (b + 1) * P)
+                nc.tensor.matmul_mx(
+                    out=acc[:, b, :],
+                    lhsT=x_code[:, cols].bitcast(FP8X4),
+                    lhsT_scale=x_scale[4 * g : P, cols],
+                    rhs=h_code.bitcast(FP8X4),
+                    rhs_scale=h_scale,
+                    start=(g == 0 and b == 0),
+                    stop=(g == PASSES - 1 and b == 3),
                 )
 
         stage = []
@@ -91,9 +116,9 @@ def tile_picked_ysedd_loss_p_kernel(
         ratio_t = []
         sums = []
         for m in range(TILES):
-            lg = keep.tile([P, 4, P], F32, name=f"log{m}")
+            lg = keep.tile([P, 4, P], F32, name=f"log{m}", tag=f"log{m}", align_bytes=64)
             nc.scalar.activation(lg[:], stage[m][:], ACT.Ln, bias=0.05)
-            rt = keep.tile([P, 4, P], F32, name=f"ratio_t{m}")
+            rt = keep.tile([P, 4, P], F32, name=f"ratio_t{m}", tag=f"ratio_t{m}", align_bytes=64)
             nc.scalar.copy(rt[:], stage[m][:])
             fixed = keep.tile([P, 4, P], F32, name=f"fixed{m}")
             nc.vector.scalar_tensor_tensor(fixed[:], lg[:], -1.0, rt[:], ALU.add, ALU.mult)
@@ -101,60 +126,39 @@ def tile_picked_ysedd_loss_p_kernel(
             turn_into(total, fixed, True, False)
             ratio_t.append(rt)
             sums.append(total)
-        warm = keep.tile([P, 1], F32, name="warm")
-        nc.scalar.activation(warm[:], lg[:, 3, P - 1 : P], ACT.Exp)
+        h_mx = quantise(h_first[:, :, :HALF], nc.vector.tensor_copy, "a0", "grouped_a0", "code_a0")
+        h_mx = h_mx + quantise(h_first[:, :, HALF:], nc.scalar.copy, "b0", "grouped_b0", "code_b0")
+        warm_exp = keep.tile([P, 1], F32, name="warm_exp", tag="warm_exp", align_bytes=64)
+        nc.scalar.activation(warm_exp[:], rt[:, 3, P - 1 : P], ACT.Exp)
 
-        x_code = []
-        for g in range(PASSES):
-            c = keep.tile([P, S], U32, name=f"x_code{g}", align_bytes=64)
-            nc.vector.tensor_copy(c[:], word_table[g][:].indirect(offsets[:]))
-            x_code.append(c)
+        acc = [psum.tile([P, 4, P], F32, name=f"acc{m}", tag="work", bufs=4) for m in range(TILES)]
+        x_code = gather_words(0, "log3")
+        for m in range(TILES):
+            multiply(acc[m], 0, x_code, *h_mx[m])
 
-        def product(m, g, acc):
-            if True:
-                grouped = keep.tile([P, P, PACK], BF16, name=f"grouped{m}{g}", tag=f"slot{m}{g}", align_bytes=64)
-                src = h_raw[m, g].rearrange("p t (c i) -> p c t i", i=4)
-                dst = grouped[:].rearrange("p (c i) t -> p c t i", i=4)
-                if m + 2 * g < 2 or (m, g) == (0, 1):
-                    nc.vector.tensor_copy(dst, src)
-                else:
-                    nc.scalar.copy(dst, src)
-                h_code = keep.tile([P, P], U32, name=f"h_code{m}{g}", align_bytes=64)
-                h_scale = keep.tile([P, P], U8, name=f"h_scale{m}{g}", align_bytes=64)
-                nc.vector.quantize_mx(
-                    out=h_code[:].bitcast(FP8X4), scales=h_scale[:], in_=grouped[:].rearrange("p c t -> p (c t)")
-                )
-                for b in range(4):
-                    cols = slice(b * P, (b + 1) * P)
-                    nc.tensor.matmul_mx(
-                        out=acc[:, b, :],
-                        lhsT=x_code[g][:, cols].bitcast(FP8X4),
-                        lhsT_scale=x_scale[4 * g : P, cols],
-                        rhs=h_code[:].bitcast(FP8X4),
-                        rhs_scale=h_scale[:],
-                        start=(g == 0 and b == 0),
-                        stop=(g == PASSES - 1 and b == 3),
-                    )
-
-        def add_terms(m, acc):
+        def add_terms(m):
             cross = keep.tile([P, 4, P], F32, name=f"cross{m}")
-            nc.vector.scalar_tensor_tensor(cross[:], acc[:], -0.7, ratio_t[m][:], ALU.mult, ALU.mult)
-            sc = keep.tile([P, 4, P], F32, name=f"sc{m}", tag="raw21" if m == 0 else f"sc{m}")
-            nc.scalar.activation(sc[:], acc[:], ACT.Exp, scale=0.7)
+            nc.vector.scalar_tensor_tensor(cross[:], acc[m][:], -0.7, ratio_t[m][:], ALU.mult, ALU.mult)
+            sc = keep.tile([P, 4, P], F32, name=f"sc{m}", align_bytes=64)
+            nc.scalar.activation(sc[:], acc[m][:], ACT.Exp, scale=0.7)
             turn_into(sums[m], cross, False, False)
             turn_into(sums[m], sc, False, True)
 
         def store(m):
-            res = keep.tile([P, S], F32, name=f"res{m}", tag="slot31" if m == 0 else f"res{m}", align_bytes=64)
+            res = keep.tile([P, S], F32, name=f"res{m}", align_bytes=64)
             nc.vector.tensor_tensor(res[:], sums[m][:].rearrange("p b c -> p (b c)"), rate_sb[:], ALU.mult)
             nc.sync.dma_start(out[m * P : (m + 1) * P, :], res[:])
 
-        acc = [psum.tile([P, 4, P], F32, name=f"acc{m}", tag="work", bufs=4) for m in range(TILES)]
-        for g in range(PASSES):
-            for m in range(TILES):
-                product(m, g, acc[m])
+        x_code = gather_words(1, "grouped_b0")
+        h_mx = quantise(h_second[0][:, :, :P], nc.vector.tensor_copy, "01", "words1", "code_01")
+        h_mx = h_mx + quantise(h_second[0][:, :, P:], nc.scalar.copy, "11", "warm_exp", "code_11")
+        h_mx = h_mx + quantise(h_second[1][:, :, :P], nc.vector.tensor_copy, "21", "warm_exp", "code_21")
+        h_mx = h_mx + quantise(h_second[1][:, :, P:], nc.scalar.copy, "31", "raw01", "code_31")
         for m in range(TILES):
-            add_terms(m, acc[m])
-            if m > 0:
-                store(m - 1)
-        store(TILES - 1)
+            multiply(acc[m], 1, x_code, *h_mx[m])
+        for m in range(TILES):
+            add_terms(m)
+            if m > 1:
+                store(m - 2)
+        store(2)
+        store(3)

from contextlib import ExitStack

import concourse.mybir as mybir
from concourse.masks import make_identity

K, T, S, V = 1024, 2048, 512, 512
FLOPS = 2 * K * V * S

F32 = mybir.dt.float32
BF16 = mybir.dt.bfloat16
I32 = mybir.dt.int32
U32 = mybir.dt.uint32
U16 = mybir.dt.uint16
U8 = mybir.dt.uint8
FP8X4 = mybir.dt.float8_e4m3fn_x4
ACT = mybir.ActivationFunctionType
ALU = mybir.AluOpType

P = 128
PACK = 4
PASSES = K // (P * PACK)
TILES = V // P
HALF = V // 2


def tile_picked_ysedd_loss_p_kernel(
    tc, x_words, x_scales, hT, ratio, rate, offs, out
):
    nc = tc.nc
    with ExitStack() as ctx:
        keep = ctx.enter_context(tc.tile_pool(name="keep", bufs=1))
        psum = ctx.enter_context(tc.psum_pool(name="psum", bufs=1))

        def load_ratio(h):
            tile = keep.tile([P, 2, S], F32, name=f"ratio{h}")
            nc.sync.dma_start(tile[:], ratio[h * HALF : (h + 1) * HALF, :].rearrange("(m p) j -> p m j", p=P))
            return tile

        def load_scale_rows():
            for q in range(4):
                nc.sync.dma_start(scale_rows[32 * q : 32 * q + 8, :], x_scales.bitcast(I32)[:, 4 * q : 4 * q + 4, :])

        def load_words(g):
            tile = keep.tile([P, T], U32, name=f"word_table{g}", tag=f"words{g}", align_bytes=64)
            nc.sync.dma_start(tile[:].bitcast(I32), x_words[g].rearrange("p n t -> p (n t)").bitcast(I32))
            return tile

        def load_hidden(g, first, count):
            raw = keep.tile([P, PACK, count * P], F32, name=f"h_raw{first}{g}", tag=f"raw{first}{g}", align_bytes=64)
            rows = hT[g * 512 : (g + 1) * 512, first * P : (first + count) * P]
            nc.sync.dma_start(raw[:], rows.rearrange("(p j) c -> p j c", j=PACK))
            return raw[:]

        offsets = keep.tile([P, S // 16], U16, name="offsets")
        scale_rows = keep.tile([P, T // 4], I32, name="scale_rows")
        rate_sb = keep.tile([P, S], F32, name="rate_sb")
        load_scale_rows()
        nc.sync.dma_start(offsets[:], offs)
        ratio_sb = [load_ratio(0), load_ratio(1)]
        h_first = load_hidden(0, 0, 4)
        word_table = [load_words(0), load_words(1)]
        h_second = [load_hidden(1, 0, 2), load_hidden(1, 2, 2)]
        nc.sync.dma_start(rate_sb[:], rate)

        scale_table = keep.tile([P, T], U8, name="scale_table", align_bytes=64)
        nc.vector.memset(scale_table[:].bitcast(I32), 0)
        identity = keep.tile([P, P], F32, name="identity")
        make_identity(nc, identity[:])
        for q in range(4):
            rows = slice(32 * q, 32 * q + 8)
            nc.vector.tensor_copy(scale_table[:].bitcast(I32)[rows, :], scale_rows[rows, :])
        x_scale = keep.tile([P, S], U8, name="x_scale", align_bytes=64)
        nc.vector.tensor_copy(x_scale[:], scale_table[:].indirect(offsets[:]))

        def quantise(raw, copy, name, grouped_tag, code_tag):
            width = raw.shape[2]
            grouped = keep.tile([P, width, PACK], BF16, name=f"grouped_{name}", tag=grouped_tag, align_bytes=64)
            copy(grouped[:].rearrange("p (c i) t -> p c t i", i=4), raw.rearrange("p t (c i) -> p c t i", i=4))
            code = keep.tile([P, width], U32, name=f"h_code_{name}", tag=code_tag, align_bytes=64)
            scale = keep.tile([P, width], U8, name=f"h_scale_{name}", align_bytes=64)
            nc.vector.quantize_mx(
                out=code[:].bitcast(FP8X4), scales=scale[:], in_=grouped[:].rearrange("p c t -> p (c t)")
            )
            return [(code[:, i : i + P], scale[:, i : i + P]) for i in range(0, width, P)]

        def gather_words(g, tag):
            code = keep.tile([P, S], U32, name=f"x_code{g}", tag=tag, align_bytes=64)
            nc.vector.tensor_copy(code[:], word_table[g][:].indirect(offsets[:]))
            return code

        def turn_into(bank, source, start, stop):
            for b in range(4):
                nc.tensor.matmul(
                    bank[:, b, :], source[:, b, :], identity[:], is_transpose=True,
                    start=start and b == 0, stop=stop and b == 3,
                )

        def multiply(acc, g, x_code, h_code, h_scale):
            for b in range(4):
                cols = slice(b * P, (b + 1) * P)
                nc.tensor.matmul_mx(
                    out=acc[:, b, :],
                    lhsT=x_code[:, cols].bitcast(FP8X4),
                    lhsT_scale=x_scale[4 * g : P, cols],
                    rhs=h_code.bitcast(FP8X4),
                    rhs_scale=h_scale,
                    start=(g == 0 and b == 0),
                    stop=(g == PASSES - 1 and b == 3),
                )

        stage = []
        for m in range(TILES):
            h, i = divmod(m, 2)
            stage.append(psum.tile([P, 4, P], F32, name=f"stage{m}", tag="work", bufs=4))
            turn_into(stage[m], ratio_sb[h][:, i, :].rearrange("p (b c) -> p b c", b=4), True, True)
        ratio_t = []
        sums = []
        for m in range(TILES):
            lg = keep.tile([P, 4, P], F32, name=f"log{m}", tag=f"log{m}", align_bytes=64)
            nc.scalar.activation(lg[:], stage[m][:], ACT.Ln, bias=0.05)
            rt = keep.tile([P, 4, P], F32, name=f"ratio_t{m}", tag=f"ratio_t{m}", align_bytes=64)
            nc.scalar.copy(rt[:], stage[m][:])
            fixed = keep.tile([P, 4, P], F32, name=f"fixed{m}")
            nc.vector.scalar_tensor_tensor(fixed[:], lg[:], -1.0, rt[:], ALU.add, ALU.mult)
            total = psum.tile([P, 4, P], F32, name=f"sum{m}")
            turn_into(total, fixed, True, False)
            ratio_t.append(rt)
            sums.append(total)
        h_mx = quantise(h_first[:, :, :HALF], nc.vector.tensor_copy, "a0", "grouped_a0", "code_a0")
        h_mx = h_mx + quantise(h_first[:, :, HALF:], nc.scalar.copy, "b0", "grouped_b0", "code_b0")
        warm_exp = keep.tile([P, 1], F32, name="warm_exp", tag="warm_exp", align_bytes=64)
        nc.scalar.activation(warm_exp[:], rt[:, 3, P - 1 : P], ACT.Exp)

        acc = [psum.tile([P, 4, P], F32, name=f"acc{m}", tag="work", bufs=4) for m in range(TILES)]
        x_code = gather_words(0, "log3")
        for m in range(TILES):
            multiply(acc[m], 0, x_code, *h_mx[m])

        def add_terms(m):
            cross = keep.tile([P, 4, P], F32, name=f"cross{m}")
            nc.vector.scalar_tensor_tensor(cross[:], acc[m][:], -0.7, ratio_t[m][:], ALU.mult, ALU.mult)
            sc = keep.tile([P, 4, P], F32, name=f"sc{m}", align_bytes=64)
            nc.scalar.activation(sc[:], acc[m][:], ACT.Exp, scale=0.7)
            turn_into(sums[m], cross, False, False)
            turn_into(sums[m], sc, False, True)

        def store(m):
            res = keep.tile([P, S], F32, name=f"res{m}", align_bytes=64)
            nc.vector.tensor_tensor(res[:], sums[m][:].rearrange("p b c -> p (b c)"), rate_sb[:], ALU.mult)
            nc.sync.dma_start(out[m * P : (m + 1) * P, :], res[:])

        x_code = gather_words(1, "grouped_b0")
        h_mx = quantise(h_second[0][:, :, :P], nc.vector.tensor_copy, "01", "words1", "code_01")
        h_mx = h_mx + quantise(h_second[0][:, :, P:], nc.scalar.copy, "11", "warm_exp", "code_11")
        h_mx = h_mx + quantise(h_second[1][:, :, :P], nc.vector.tensor_copy, "21", "warm_exp", "code_21")
        h_mx = h_mx + quantise(h_second[1][:, :, P:], nc.scalar.copy, "31", "raw01", "code_31")
        for m in range(TILES):
            multiply(acc[m], 1, x_code, *h_mx[m])
        for m in range(TILES):
            add_terms(m)
            if m > 1:
                store(m - 2)
        store(2)
        store(3)
